import numpy as np
import ml_dtypes


def mxq(x, axis, fmt="e4m3"):
    dtype, down = {"e4m3": (ml_dtypes.float8_e4m3fn, 7), "e5m2": (ml_dtypes.float8_e5m2, 14)}[fmt]
    v = np.moveaxis(np.asarray(x, np.float32).astype(ml_dtypes.bfloat16).astype(np.float64), axis, -1)
    blocks = v.reshape(v.shape[:-1] + (-1, 32))
    amax = np.abs(blocks).max(-1, keepdims=True)
    byte = np.maximum(np.where(amax > 0, np.frexp(amax)[1] - 1 + 127, 0) - down, 1)
    scale = np.exp2(byte - 127.0)
    codes = (blocks / scale).astype(np.float32).astype(dtype).astype(np.float64)
    return np.moveaxis((codes * scale).reshape(v.shape), -1, axis)


WIDE = False


def mx_kscale(k):
    if not WIDE:
        return np.ones(k)
    levels = np.array([10, -10, 5, -5, 0])
    if k % 512:
        return np.exp2(np.random.permutation(np.resize(levels, k // 32))).repeat(32)
    a = np.empty((k // 512, 16))
    for p in range(k // 512):
        a[p, :8] = np.random.permutation(np.resize(levels, 8))
        for g in range(8):
            far = levels[np.abs(levels - a[p, g]) >= 10]
            a[p, g + 8] = far[np.random.randint(len(far))]
    return np.exp2(a.ravel()).repeat(32)


def f64(x):
    return np.asarray(x).astype(np.float64)


def striped(idx):
    return np.tile(np.asarray(idx).reshape(-1, 16).T, (8, 1)).astype(np.uint16)


def unstriped(offs):
    return offs[:16].T.reshape(-1).astype(np.int64)


E2M1 = np.array([0.0, 0.5, 1.0, 1.5, 2.0, 3.0, 4.0, 6.0, -0.0, -0.5, -1.0, -1.5, -2.0, -3.0, -4.0, -6.0])


def pack_weight(w, fmt):
    k, n = w.shape
    w = f64(np.asarray(w, np.float32).astype(ml_dtypes.bfloat16)).reshape(k // 32, 32, n)
    amax = np.abs(w).max(1)
    if fmt == "e4m3":
        byte = np.frexp(amax)[1] - 1 + 127 - 7
    else:
        mant, ex = np.frexp(amax / 6.0)
        byte = np.where(mant > 0.5, ex, ex - 1) + 127
    byte = np.clip(np.where(amax > 0, byte, 1), 1, 254)
    scaled = (w * np.exp2(127.0 - byte)[:, None, :]).reshape(k, n).astype(np.float32)
    by_word = np.ascontiguousarray(scaled.reshape(k // 512, 128, 4, n).transpose(0, 1, 3, 2))
    if fmt == "e4m3":
        words = by_word.astype(ml_dtypes.float8_e4m3fn).view(np.uint8)
    else:
        c = by_word.astype(ml_dtypes.float4_e2m1fn).view(np.uint8) & 0xF
        words = (c[..., 0::2] | (c[..., 1::2] << 4)).reshape(k // 512, 128, 2 * n)
    return np.ascontiguousarray(words), np.ascontiguousarray(byte.astype(np.uint8).reshape(k // 512, 16, n))


def unpack_weight(words, scales, fmt):
    g, _, n = scales.shape
    words = np.ascontiguousarray(words).reshape(g, 128, n, -1)
    if fmt == "e4m3":
        vals = words.view(ml_dtypes.float8_e4m3fn).astype(np.float64)
    else:
        nib = np.empty((g, 128, n, 4), np.uint8)
        nib[..., 0::2] = words & 0xF
        nib[..., 1::2] = words >> 4
        vals = E2M1[nib]
    vals = vals * np.repeat(np.exp2(scales.astype(np.float64) - 127.0), 8, axis=1)[..., None]
    return vals.transpose(0, 1, 3, 2).reshape(g * 512, n)


D, T, Q, V = 512, 1024, 256, 2048


def setup_inputs():
    n = np.random.standard_normal
    idx = np.random.permutation(T)[:Q]
    idx2 = np.random.permutation(T)[:Q]
    idx3 = np.random.permutation(T)[:Q]
    fd = mx_kscale(D)
    candp = pack_weight(n((D, V)) / fd[:, None], "e2m1")
    return {
        "ent": (n((D, T)) * 1 / np.sqrt(D)).astype(np.float32),
        "fsc": (np.random.uniform(0.5, 1.5, (D, 1)) * fd[:, None]).astype(np.float32),
        "cand_words": candp[0],
        "cand_scales": candp[1],
        "temp": (np.random.uniform(1.5, 3.0, (Q, 1))).astype(np.float32),
        "offs": striped(idx),
        "offs2": striped(idx2),
        "offs3": striped(idx3),
    }


def reference(ent, fsc, cand_words, cand_scales, temp, offs, offs2, offs3):
    idx = unstriped(offs)
    idx2 = unstriped(offs2)
    idx3 = unstriped(offs3)
    candu = unpack_weight(cand_words, cand_scales, "e2m1")
    sv = (f64(ent)[:, idx2] - f64(ent)[:, idx] + f64(ent)[:, idx3]) * f64(fsc)
    svq = mxq(sv, 0, "e4m3")
    a = svq.T @ candu
    s = a / f64(temp)
    p = np.exp(s - np.max(s, axis=1, keepdims=True))
    y = p / np.sum(p, axis=1, keepdims=True) * 2048.0
    return y

@@ -1,0 +1,134 @@
+from contextlib import ExitStack
+
+import concourse.mybir as mybir
+
+D, T, Q, V = 512, 1024, 256, 2048
+FLOPS = 2 * D * Q * V
+
+F32 = mybir.dt.float32
+BF16 = mybir.dt.bfloat16
+I32 = mybir.dt.int32
+U32 = mybir.dt.uint32
+U16 = mybir.dt.uint16
+U8 = mybir.dt.uint8
+FP8X4 = mybir.dt.float8_e4m3fn_x4
+FP4X4 = mybir.dt.float4_e2m1fn_x4
+ALU = mybir.AluOpType
+ACT = mybir.ActivationFunctionType
+AX = mybir.AxisListType
+
+P = 128
+PACK = 4
+BANK = 512
+HALVES = Q // P
+CHUNKS = V // BANK
+LIST_COLS = P // 16
+OUT_SCALE = 2048.0
+
+
+def tile_attend_analogies_kernel(tc, ent, fsc, cand_words, cand_scales, temp, offs, offs2, offs3, out):
+    nc = tc.nc
+    with ExitStack() as ctx:
+        keep = ctx.enter_context(tc.tile_pool(name="keep", bufs=1))
+        psum = ctx.enter_context(tc.psum_pool(name="psum", bufs=1))
+
+        first = keep.tile([P, Q // 16], U16, name="first")
+        second = keep.tile([P, Q // 16], U16, name="second")
+        third = keep.tile([P, Q // 16], U16, name="third")
+        planes = [keep.tile([P, T], F32, name="plane%d" % t) for t in range(PACK)]
+        feature_scale = keep.tile([P, PACK], F32, name="feature_scale")
+        temps = keep.tile([P, HALVES], F32, name="temps")
+        words = keep.tile([P, 2 * V], U8, name="words", align_bytes=64)
+        scales = keep.tile([P, V], U8, name="scales", align_bytes=64)
+
+        ent_planes = ent.rearrange("(p t) n -> t p n", t=PACK)
+        nc.gpsimd.memset(scales[:].bitcast(I32), 0)
+        nc.sync.dma_start(first[:], offs)
+        nc.sync.dma_start(out=planes[0][:], in_=ent_planes[0])
+        nc.sync.dma_start(second[:], offs2)
+        nc.sync.dma_start(third[:], offs3)
+        nc.sync.dma_start(out=feature_scale[:], in_=fsc.rearrange("(p t) o -> p (t o)", t=PACK))
+        for t in range(1, PACK):
+            nc.sync.dma_start(out=planes[t][:], in_=ent_planes[t])
+        nc.sync.dma_start(out=words[:].bitcast(I32), in_=cand_words[0].bitcast(I32))
+        for g in range(4):
+            nc.sync.dma_start(
+                out=scales[32 * g : 32 * g + 4, :].bitcast(I32),
+                in_=cand_scales[0, 4 * g : 4 * g + 4, :].bitcast(I32),
+            )
+        with nc.allow_non_contiguous_dma(reason="one temperature a partition for each half"):
+            nc.sync.dma_start(out=temps[:], in_=temp.rearrange("(h p) o -> p (h o)", h=HALVES))
+
+        sought = [keep.tile([P, P, PACK], BF16, name="sought%d" % h, align_bytes=64) for h in range(HALVES)]
+        for t in range(PACK):
+            for h in range(HALVES):
+                cols = slice(h * LIST_COLS, (h + 1) * LIST_COLS)
+                picked = keep.tile([P, P], F32, name="picked%d_%d" % (h, t))
+                diff = keep.tile([P, P], F32, name="diff%d_%d" % (h, t))
+                total = keep.tile([P, P], F32, name="total%d_%d" % (h, t))
+                nc.vector.tensor_copy(picked[:], planes[t][:].indirect(first[:, cols]))
+                nc.vector.tensor_tensor(diff[:], planes[t][:].indirect(second[:, cols]), picked[:], ALU.subtract)
+                nc.vector.tensor_tensor(total[:], planes[t][:].indirect(third[:, cols]), diff[:], ALU.add)
+                nc.scalar.activation(
+                    out=sought[h][:, :, t], in_=total[:], func=ACT.Copy, scale=feature_scale[:, t : t + 1]
+                )
+
+        inv_temp = keep.tile([P, HALVES], F32, name="inv_temp")
+        neg_inv_temp = keep.tile([P, HALVES], F32, name="neg_inv_temp")
+        nc.vector.reciprocal(inv_temp[:], temps[:])
+        nc.vector.tensor_scalar(neg_inv_temp[:], inv_temp[:], -1.0, None, ALU.mult)
+
+        banks = {}
+        for h in range(HALVES):
+            codes = keep.tile([P, P], U32, name="codes%d" % h, align_bytes=64)
+            code_scales = keep.tile([P, P], U8, name="code_scales%d" % h, align_bytes=64)
+            nc.vector.quantize_mx(
+                out=codes[:].bitcast(FP8X4),
+                scales=code_scales[:],
+                in_=sought[h][:].rearrange("p q t -> p (q t)"),
+            )
+            for c in range(CHUNKS):
+                bank = psum.tile([P, BANK], F32, name="bank%d_%d" % (h, c))
+                nc.tensor.matmul_mx(
+                    out=bank[:],
+                    lhsT=codes[:].bitcast(FP8X4),
+                    lhsT_scale=code_scales[:],
+                    rhs=words[:, 2 * BANK * c : 2 * BANK * (c + 1)].bitcast(FP4X4),
+                    rhs_scale=scales[:, BANK * c : BANK * (c + 1)],
+                    start=True,
+                    stop=True,
+                )
+                banks[h, c] = bank
+
+        for h in range(HALVES):
+            neg_max = keep.tile([P, CHUNKS], F32, name="neg_max%d" % h)
+            sums = keep.tile([P, CHUNKS], F32, name="sums%d" % h)
+            weights = []
+            for c in range(CHUNKS):
+                neg_s = keep.tile([P, BANK], F32, name="neg_s%d_%d" % (h, c))
+                weight = keep.tile([P, BANK], F32, name="weight%d_%d" % (h, c))
+                nc.vector.tensor_scalar(
+                    neg_s[:], banks[h, c][:], neg_inv_temp[:, h : h + 1], None, ALU.mult, ALU.min,
+                    accum_out=neg_max[:, c : c + 1],
+                )
+                nc.scalar.activation(
+                    out=weight[:], in_=neg_s[:], func=ACT.Exp, bias=neg_max[:, c : c + 1], scale=-1.0,
+                    accum_out=sums[:, c : c + 1],
+                )
+                weights.append(weight)
+            row_neg_max = keep.tile([P, 1], F32, name="row_neg_max%d" % h)
+            factor = keep.tile([P, CHUNKS], F32, name="factor%d" % h)
+            terms = keep.tile([P, CHUNKS], F32, name="terms%d" % h)
+            row_sum = keep.tile([P, 1], F32, name="row_sum%d" % h)
+            norm = keep.tile([P, 1], F32, name="norm%d" % h)
+            nc.vector.tensor_reduce(row_neg_max[:], neg_max[:], AX.X, ALU.min)
+            nc.scalar.activation(out=factor[:], in_=neg_max[:], func=ACT.Exp, bias=row_neg_max[:], scale=-1.0)
+            nc.vector.scalar_tensor_tensor(
+                terms[:], factor[:], 1.0 / OUT_SCALE, sums[:], ALU.mult, ALU.mult, accum_out=row_sum[:]
+            )
+            nc.vector.reciprocal(norm[:], row_sum[:])
+            engine = nc.gpsimd if h == 0 else nc.vector
+            for c in range(CHUNKS):
+                result = keep.tile([P, BANK], F32, name="result%d_%d" % (h, c))
+                engine.tensor_scalar(result[:], weights[c][:], factor[:, c : c + 1], norm[:], ALU.mult, ALU.mult)
+                nc.sync.dma_start(out=out[h * P : (h + 1) * P, c * BANK : (c + 1) * BANK], in_=result[:])

@@ -24,6 +24,7 @@ HALVES = Q // P
 CHUNKS = V // BANK
 LIST_COLS = P // 16
 OUT_SCALE = 2048.0
+SPLIT = 896
 
 
 def tile_attend_analogies_kernel(tc, ent, fsc, cand_words, cand_scales, temp, offs, offs2, offs3, out):
@@ -48,8 +49,10 @@ def tile_attend_analogies_kernel(tc, ent, fsc, cand_words, cand_scales, temp, of
         nc.sync.dma_start(second[:], offs2)
         nc.sync.dma_start(third[:], offs3)
         nc.sync.dma_start(out=feature_scale[:], in_=fsc.rearrange("(p t) o -> p (t o)", t=PACK))
-        for t in range(1, PACK):
-            nc.sync.dma_start(out=planes[t][:], in_=ent_planes[t])
+        nc.sync.dma_start(out=planes[1][:], in_=ent_planes[1])
+        nc.sync.dma_start(out=planes[2][:, :SPLIT], in_=ent_planes[2][:, :SPLIT])
+        nc.sync.dma_start(out=planes[3][:], in_=ent_planes[3])
+        nc.sync.dma_start(out=planes[2][:, SPLIT:], in_=ent_planes[2][:, SPLIT:])
         nc.sync.dma_start(out=words[:].bitcast(I32), in_=cand_words[0].bitcast(I32))
         for g in range(4):
             nc.sync.dma_start(
@@ -59,27 +62,24 @@ def tile_attend_analogies_kernel(tc, ent, fsc, cand_words, cand_scales, temp, of
         with nc.allow_non_contiguous_dma(reason="one temperature a partition for each half"):
             nc.sync.dma_start(out=temps[:], in_=temp.rearrange("(h p) o -> p (h o)", h=HALVES))
 
-        sought = [keep.tile([P, P, PACK], BF16, name="sought%d" % h, align_bytes=64) for h in range(HALVES)]
-        for t in range(PACK):
-            for h in range(HALVES):
-                cols = slice(h * LIST_COLS, (h + 1) * LIST_COLS)
-                picked = keep.tile([P, P], F32, name="picked%d_%d" % (h, t))
-                diff = keep.tile([P, P], F32, name="diff%d_%d" % (h, t))
-                total = keep.tile([P, P], F32, name="total%d_%d" % (h, t))
-                nc.vector.tensor_copy(picked[:], planes[t][:].indirect(first[:, cols]))
-                nc.vector.tensor_tensor(diff[:], planes[t][:].indirect(second[:, cols]), picked[:], ALU.subtract)
-                nc.vector.tensor_tensor(total[:], planes[t][:].indirect(third[:, cols]), diff[:], ALU.add)
-                nc.scalar.activation(
-                    out=sought[h][:, :, t], in_=total[:], func=ACT.Copy, scale=feature_scale[:, t : t + 1]
-                )
+        sought = [
+            keep.tile([P, P, PACK], BF16, name="sought%d" % h, tag="sought%d" % h, align_bytes=64)
+            for h in range(HALVES)
+        ]
 
-        inv_temp = keep.tile([P, HALVES], F32, name="inv_temp")
-        neg_inv_temp = keep.tile([P, HALVES], F32, name="neg_inv_temp")
-        nc.vector.reciprocal(inv_temp[:], temps[:])
-        nc.vector.tensor_scalar(neg_inv_temp[:], inv_temp[:], -1.0, None, ALU.mult)
+        def combine(h, t, picked_tag, diff_tag):
+            cols = slice(h * LIST_COLS, (h + 1) * LIST_COLS)
+            picked = keep.tile([P, P], F32, name="picked%d_%d" % (h, t), tag=picked_tag, align_bytes=64)
+            diff = keep.tile([P, P], F32, name="diff%d_%d" % (h, t), tag=diff_tag, align_bytes=64)
+            total = keep.tile([P, P], F32, name="total%d_%d" % (h, t))
+            nc.vector.tensor_copy(picked[:], planes[t][:].indirect(first[:, cols]))
+            nc.vector.tensor_tensor(diff[:], planes[t][:].indirect(second[:, cols]), picked[:], ALU.subtract)
+            nc.vector.tensor_tensor(total[:], planes[t][:].indirect(third[:, cols]), diff[:], ALU.add)
+            nc.scalar.activation(out=sought[h][:, :, t], in_=total[:], func=ACT.Copy, scale=feature_scale[:, t : t + 1])
 
         banks = {}
-        for h in range(HALVES):
+
+        def score(h):
             codes = keep.tile([P, P], U32, name="codes%d" % h, align_bytes=64)
             code_scales = keep.tile([P, P], U8, name="code_scales%d" % h, align_bytes=64)
             nc.vector.quantize_mx(
@@ -100,9 +100,27 @@ def tile_attend_analogies_kernel(tc, ent, fsc, cand_words, cand_scales, temp, of
                 )
                 banks[h, c] = bank
 
+        for h, t in ((0, 0), (1, 0), (0, 1), (1, 1), (0, 3), (0, 2)):
+            combine(h, t, "picked%d_%d" % (h, t), "diff%d_%d" % (h, t))
+
+        inv_temp = keep.tile([P, HALVES], F32, name="inv_temp")
+        neg_inv_temp = keep.tile([P, HALVES], F32, name="neg_inv_temp")
+        nc.vector.reciprocal(inv_temp[:], temps[:])
+        nc.vector.tensor_scalar(neg_inv_temp[:], inv_temp[:], -1.0, None, ALU.mult)
+
+        score(0)
+        combine(1, 3, "diff0_3", "diff1_3")
+        combine(1, 2, "diff0_2", "sought0")
+        score(1)
+
         for h in range(HALVES):
             neg_max = keep.tile([P, CHUNKS], F32, name="neg_max%d" % h)
             sums = keep.tile([P, CHUNKS], F32, name="sums%d" % h)
+            row_neg_max = keep.tile([P, 1], F32, name="row_neg_max%d" % h)
+            factor = keep.tile([P, CHUNKS], F32, name="factor%d" % h)
+            terms = keep.tile([P, CHUNKS], F32, name="terms%d" % h)
+            row_sum = keep.tile([P, 1], F32, name="row_sum%d" % h)
+            norm = keep.tile([P, 1], F32, name="norm%d" % h)
             weights = []
             for c in range(CHUNKS):
                 neg_s = keep.tile([P, BANK], F32, name="neg_s%d_%d" % (h, c))
@@ -111,24 +129,23 @@ def tile_attend_analogies_kernel(tc, ent, fsc, cand_words, cand_scales, temp, of
                     neg_s[:], banks[h, c][:], neg_inv_temp[:, h : h + 1], None, ALU.mult, ALU.min,
                     accum_out=neg_max[:, c : c + 1],
                 )
+                if c == CHUNKS - 1:
+                    nc.vector.tensor_reduce(row_neg_max[:], neg_max[:], AX.X, ALU.min)
+                    nc.scalar.activation(
+                        out=factor[:], in_=neg_max[:], func=ACT.Exp, bias=row_neg_max[:], scale=-1.0
+                    )
                 nc.scalar.activation(
                     out=weight[:], in_=neg_s[:], func=ACT.Exp, bias=neg_max[:, c : c + 1], scale=-1.0,
                     accum_out=sums[:, c : c + 1],
                 )
                 weights.append(weight)
-            row_neg_max = keep.tile([P, 1], F32, name="row_neg_max%d" % h)
-            factor = keep.tile([P, CHUNKS], F32, name="factor%d" % h)
-            terms = keep.tile([P, CHUNKS], F32, name="terms%d" % h)
-            row_sum = keep.tile([P, 1], F32, name="row_sum%d" % h)
-            norm = keep.tile([P, 1], F32, name="norm%d" % h)
-            nc.vector.tensor_reduce(row_neg_max[:], neg_max[:], AX.X, ALU.min)
-            nc.scalar.activation(out=factor[:], in_=neg_max[:], func=ACT.Exp, bias=row_neg_max[:], scale=-1.0)
             nc.vector.scalar_tensor_tensor(
                 terms[:], factor[:], 1.0 / OUT_SCALE, sums[:], ALU.mult, ALU.mult, accum_out=row_sum[:]
             )
             nc.vector.reciprocal(norm[:], row_sum[:])
             engine = nc.gpsimd if h == 0 else nc.vector
+            queue = nc.sync if h == 0 else nc.scalar
             for c in range(CHUNKS):
                 result = keep.tile([P, BANK], F32, name="result%d_%d" % (h, c))
                 engine.tensor_scalar(result[:], weights[c][:], factor[:, c : c + 1], norm[:], ALU.mult, ALU.mult)
-                nc.sync.dma_start(out=out[h * P : (h + 1) * P, c * BANK : (c + 1) * BANK], in_=result[:])
+                queue.dma_start(out=out[h * P : (h + 1) * P, c * BANK : (c + 1) * BANK], in_=result[:])

@@ -1,4 +1,5 @@
 from contextlib import ExitStack
+from itertools import accumulate
 
 import concourse.mybir as mybir
 
@@ -27,6 +28,11 @@ OUT_SCALE = 2048.0
 SPLIT = 896
 
 
+def spans(widths):
+    ends = list(accumulate(widths))
+    return list(zip([0] + ends[:-1], ends))
+
+
 def tile_attend_analogies_kernel(tc, ent, fsc, cand_words, cand_scales, temp, offs, offs2, offs3, out):
     nc = tc.nc
     with ExitStack() as ctx:
@@ -44,8 +50,8 @@ def tile_attend_analogies_kernel(tc, ent, fsc, cand_words, cand_scales, temp, of
 
         ent_planes = ent.rearrange("(p t) n -> t p n", t=PACK)
         nc.gpsimd.memset(scales[:].bitcast(I32), 0)
-        nc.sync.dma_start(first[:], offs)
         nc.sync.dma_start(out=planes[0][:], in_=ent_planes[0])
+        nc.sync.dma_start(first[:], offs)
         nc.sync.dma_start(second[:], offs2)
         nc.sync.dma_start(third[:], offs3)
         nc.sync.dma_start(out=feature_scale[:], in_=fsc.rearrange("(p t) o -> p (t o)", t=PACK))
@@ -79,8 +85,8 @@ def tile_attend_analogies_kernel(tc, ent, fsc, cand_words, cand_scales, temp, of
 
         banks = {}
 
-        def score(h):
-            codes = keep.tile([P, P], U32, name="codes%d" % h, align_bytes=64)
+        def score(h, codes_tag):
+            codes = keep.tile([P, P], U32, name="codes%d" % h, tag=codes_tag, align_bytes=64)
             code_scales = keep.tile([P, P], U8, name="code_scales%d" % h, align_bytes=64)
             nc.vector.quantize_mx(
                 out=codes[:].bitcast(FP8X4),
@@ -108,44 +114,64 @@ def tile_attend_analogies_kernel(tc, ent, fsc, cand_words, cand_scales, temp, of
         nc.vector.reciprocal(inv_temp[:], temps[:])
         nc.vector.tensor_scalar(neg_inv_temp[:], inv_temp[:], -1.0, None, ALU.mult)
 
-        score(0)
+        score(0, "codes0")
         combine(1, 3, "diff0_3", "diff1_3")
         combine(1, 2, "diff0_2", "sought0")
-        score(1)
 
-        for h in range(HALVES):
-            neg_max = keep.tile([P, CHUNKS], F32, name="neg_max%d" % h)
-            sums = keep.tile([P, CHUNKS], F32, name="sums%d" % h)
-            row_neg_max = keep.tile([P, 1], F32, name="row_neg_max%d" % h)
-            factor = keep.tile([P, CHUNKS], F32, name="factor%d" % h)
-            terms = keep.tile([P, CHUNKS], F32, name="terms%d" % h)
-            row_sum = keep.tile([P, 1], F32, name="row_sum%d" % h)
-            norm = keep.tile([P, 1], F32, name="norm%d" % h)
-            weights = []
-            for c in range(CHUNKS):
-                neg_s = keep.tile([P, BANK], F32, name="neg_s%d_%d" % (h, c))
-                weight = keep.tile([P, BANK], F32, name="weight%d_%d" % (h, c))
-                nc.vector.tensor_scalar(
-                    neg_s[:], banks[h, c][:], neg_inv_temp[:, h : h + 1], None, ALU.mult, ALU.min,
-                    accum_out=neg_max[:, c : c + 1],
-                )
-                if c == CHUNKS - 1:
-                    nc.vector.tensor_reduce(row_neg_max[:], neg_max[:], AX.X, ALU.min)
-                    nc.scalar.activation(
-                        out=factor[:], in_=neg_max[:], func=ACT.Exp, bias=row_neg_max[:], scale=-1.0
-                    )
-                nc.scalar.activation(
-                    out=weight[:], in_=neg_s[:], func=ACT.Exp, bias=neg_max[:, c : c + 1], scale=-1.0,
-                    accum_out=sums[:, c : c + 1],
-                )
-                weights.append(weight)
-            nc.vector.scalar_tensor_tensor(
-                terms[:], factor[:], 1.0 / OUT_SCALE, sums[:], ALU.mult, ALU.mult, accum_out=row_sum[:]
+        pieces = [spans(widths) for widths in ((256, 256, 512, 512, 512), (512, 512, 512, 512))]
+        neg_max = [keep.tile([P, len(pieces[h])], F32, name="neg_max%d" % h) for h in range(HALVES)]
+        sums = [keep.tile([P, len(pieces[h])], F32, name="sums%d" % h) for h in range(HALVES)]
+        factor = [keep.tile([P, len(pieces[h])], F32, name="factor%d" % h) for h in range(HALVES)]
+        row_sum = [keep.tile([P, 1], F32, name="row_sum%d" % h) for h in range(HALVES)]
+        norm = [keep.tile([P, 1], F32, name="norm%d" % h) for h in range(HALVES)]
+        weights = {}
+
+        def weigh(h, i):
+            lo, hi = pieces[h][i]
+            c = lo // BANK
+            neg_s = keep.tile([P, hi - lo], F32, name="neg_s%d_%d" % (h, i), tag="neg_s%d_%d" % (h, i), align_bytes=64)
+            weight = keep.tile([P, hi - lo], F32, name="weight%d_%d" % (h, i))
+            nc.vector.tensor_scalar(
+                neg_s[:], banks[h, c][:, lo - c * BANK : hi - c * BANK], neg_inv_temp[:, h : h + 1], None,
+                ALU.mult, ALU.min, accum_out=neg_max[h][:, i : i + 1],
             )
-            nc.vector.reciprocal(norm[:], row_sum[:])
-            engine = nc.gpsimd if h == 0 else nc.vector
-            queue = nc.sync if h == 0 else nc.scalar
-            for c in range(CHUNKS):
-                result = keep.tile([P, BANK], F32, name="result%d_%d" % (h, c))
-                engine.tensor_scalar(result[:], weights[c][:], factor[:, c : c + 1], norm[:], ALU.mult, ALU.mult)
-                queue.dma_start(out=out[h * P : (h + 1) * P, c * BANK : (c + 1) * BANK], in_=result[:])
+            if i == len(pieces[h]) - 1:
+                row_neg_max = keep.tile([P, 1], F32, name="row_neg_max%d" % h)
+                nc.vector.tensor_reduce(row_neg_max[:], neg_max[h][:], AX.X, ALU.min)
+                nc.scalar.activation(
+                    out=factor[h][:], in_=neg_max[h][:], func=ACT.Exp, bias=row_neg_max[:], scale=-1.0
+                )
+            nc.scalar.activation(
+                out=weight[:], in_=neg_s[:], func=ACT.Exp, bias=neg_max[h][:, i : i + 1], scale=-1.0,
+                accum_out=sums[h][:, i : i + 1],
+            )
+            weights[h, i] = weight
+
+        def add_up(h):
+            terms = keep.tile([P, len(pieces[h])], F32, name="terms%d" % h)
+            nc.vector.scalar_tensor_tensor(
+                terms[:], factor[h][:], 1.0 / OUT_SCALE, sums[h][:], ALU.mult, ALU.mult, accum_out=row_sum[h][:]
+            )
+            nc.vector.reciprocal(norm[h][:], row_sum[h][:])
+
+        def finish(h, queue):
+            for start, end in spans((512, 512, 1024)):
+                result = keep.tile([P, end - start], F32, name="result%d_%d" % (h, start))
+                for i, (lo, hi) in enumerate(pieces[h]):
+                    if start <= lo < end:
+                        nc.vector.tensor_scalar(
+                            result[:, lo - start : hi - start], weights[h, i][:], factor[h][:, i : i + 1], norm[h][:],
+                            ALU.mult, ALU.mult,
+                        )
+                queue.dma_start(out=out[h * P : (h + 1) * P, start:end], in_=result[:])
+
+        weigh(0, 0)
+        score(1, "neg_s0_0")
+        for i in range(1, len(pieces[0])):
+            weigh(0, i)
+        add_up(0)
+        for i in range(len(pieces[1])):
+            weigh(1, i)
+        add_up(1)
+        finish(0, nc.sync)
+        finish(1, nc.scalar)

@@ -51,9 +51,9 @@ def tile_attend_analogies_kernel(tc, ent, fsc, cand_words, cand_scales, temp, of
         ent_planes = ent.rearrange("(p t) n -> t p n", t=PACK)
         nc.gpsimd.memset(scales[:].bitcast(I32), 0)
         nc.sync.dma_start(out=planes[0][:], in_=ent_planes[0])
-        nc.sync.dma_start(first[:], offs)
         nc.sync.dma_start(second[:], offs2)
         nc.sync.dma_start(third[:], offs3)
+        nc.sync.dma_start(first[:], offs)
         nc.sync.dma_start(out=feature_scale[:], in_=fsc.rearrange("(p t) o -> p (t o)", t=PACK))
         nc.sync.dma_start(out=planes[1][:], in_=ent_planes[1])
         nc.sync.dma_start(out=planes[2][:, :SPLIT], in_=ent_planes[2][:, :SPLIT])
@@ -78,9 +78,9 @@ def tile_attend_analogies_kernel(tc, ent, fsc, cand_words, cand_scales, temp, of
             picked = keep.tile([P, P], F32, name="picked%d_%d" % (h, t), tag=picked_tag, align_bytes=64)
             diff = keep.tile([P, P], F32, name="diff%d_%d" % (h, t), tag=diff_tag, align_bytes=64)
             total = keep.tile([P, P], F32, name="total%d_%d" % (h, t))
-            nc.vector.tensor_copy(picked[:], planes[t][:].indirect(first[:, cols]))
-            nc.vector.tensor_tensor(diff[:], planes[t][:].indirect(second[:, cols]), picked[:], ALU.subtract)
-            nc.vector.tensor_tensor(total[:], planes[t][:].indirect(third[:, cols]), diff[:], ALU.add)
+            nc.vector.tensor_copy(picked[:], planes[t][:].indirect(second[:, cols]))
+            nc.vector.tensor_tensor(diff[:], planes[t][:].indirect(third[:, cols]), picked[:], ALU.add)
+            nc.vector.tensor_tensor(total[:], planes[t][:].indirect(first[:, cols]), diff[:], ALU.subtract)
             nc.scalar.activation(out=sought[h][:, :, t], in_=total[:], func=ACT.Copy, scale=feature_scale[:, t : t + 1])
 
         banks = {}
@@ -110,15 +110,13 @@ def tile_attend_analogies_kernel(tc, ent, fsc, cand_words, cand_scales, temp, of
             combine(h, t, "picked%d_%d" % (h, t), "diff%d_%d" % (h, t))
 
         inv_temp = keep.tile([P, HALVES], F32, name="inv_temp")
-        neg_inv_temp = keep.tile([P, HALVES], F32, name="neg_inv_temp")
         nc.vector.reciprocal(inv_temp[:], temps[:])
-        nc.vector.tensor_scalar(neg_inv_temp[:], inv_temp[:], -1.0, None, ALU.mult)
 
         score(0, "codes0")
         combine(1, 3, "diff0_3", "diff1_3")
         combine(1, 2, "diff0_2", "sought0")
 
-        pieces = [spans(widths) for widths in ((256, 256, 512, 512, 512), (512, 512, 512, 512))]
+        pieces = [spans(widths) for widths in ((128, 384, 512, 512, 512), (512, 512, 512, 512))]
         neg_max = [keep.tile([P, len(pieces[h])], F32, name="neg_max%d" % h) for h in range(HALVES)]
         sums = [keep.tile([P, len(pieces[h])], F32, name="sums%d" % h) for h in range(HALVES)]
         factor = [keep.tile([P, len(pieces[h])], F32, name="factor%d" % h) for h in range(HALVES)]
@@ -132,7 +130,7 @@ def tile_attend_analogies_kernel(tc, ent, fsc, cand_words, cand_scales, temp, of
             neg_s = keep.tile([P, hi - lo], F32, name="neg_s%d_%d" % (h, i), tag="neg_s%d_%d" % (h, i), align_bytes=64)
             weight = keep.tile([P, hi - lo], F32, name="weight%d_%d" % (h, i))
             nc.vector.tensor_scalar(
-                neg_s[:], banks[h, c][:, lo - c * BANK : hi - c * BANK], neg_inv_temp[:, h : h + 1], None,
+                neg_s[:], banks[h, c][:, lo - c * BANK : hi - c * BANK], inv_temp[:, h : h + 1], None,
                 ALU.mult, ALU.min, accum_out=neg_max[h][:, i : i + 1],
             )
             if i == len(pieces[h]) - 1:

from contextlib import ExitStack
from itertools import accumulate

import concourse.mybir as mybir

D, T, Q, V = 512, 1024, 256, 2048
FLOPS = 2 * D * Q * V

F32 = mybir.dt.float32
BF16 = mybir.dt.bfloat16
I32 = mybir.dt.int32
U32 = mybir.dt.uint32
U16 = mybir.dt.uint16
U8 = mybir.dt.uint8
FP8X4 = mybir.dt.float8_e4m3fn_x4
FP4X4 = mybir.dt.float4_e2m1fn_x4
ALU = mybir.AluOpType
ACT = mybir.ActivationFunctionType
AX = mybir.AxisListType

P = 128
PACK = 4
BANK = 512
HALVES = Q // P
CHUNKS = V // BANK
LIST_COLS = P // 16
OUT_SCALE = 2048.0
SPLIT = 896


def spans(widths):
    ends = list(accumulate(widths))
    return list(zip([0] + ends[:-1], ends))


def tile_attend_analogies_kernel(tc, ent, fsc, cand_words, cand_scales, temp, offs, offs2, offs3, out):
    nc = tc.nc
    with ExitStack() as ctx:
        keep = ctx.enter_context(tc.tile_pool(name="keep", bufs=1))
        psum = ctx.enter_context(tc.psum_pool(name="psum", bufs=1))

        first = keep.tile([P, Q // 16], U16, name="first")
        second = keep.tile([P, Q // 16], U16, name="second")
        third = keep.tile([P, Q // 16], U16, name="third")
        planes = [keep.tile([P, T], F32, name="plane%d" % t) for t in range(PACK)]
        feature_scale = keep.tile([P, PACK], F32, name="feature_scale")
        temps = keep.tile([P, HALVES], F32, name="temps")
        words = keep.tile([P, 2 * V], U8, name="words", align_bytes=64)
        scales = keep.tile([P, V], U8, name="scales", align_bytes=64)

        ent_planes = ent.rearrange("(p t) n -> t p n", t=PACK)
        nc.gpsimd.memset(scales[:].bitcast(I32), 0)
        nc.sync.dma_start(out=planes[0][:], in_=ent_planes[0])
        nc.sync.dma_start(second[:], offs2)
        nc.sync.dma_start(third[:], offs3)
        nc.sync.dma_start(first[:], offs)
        nc.sync.dma_start(out=feature_scale[:], in_=fsc.rearrange("(p t) o -> p (t o)", t=PACK))
        nc.sync.dma_start(out=planes[1][:], in_=ent_planes[1])
        nc.sync.dma_start(out=planes[2][:, :SPLIT], in_=ent_planes[2][:, :SPLIT])
        nc.sync.dma_start(out=planes[3][:], in_=ent_planes[3])
        nc.sync.dma_start(out=planes[2][:, SPLIT:], in_=ent_planes[2][:, SPLIT:])
        nc.sync.dma_start(out=words[:].bitcast(I32), in_=cand_words[0].bitcast(I32))
        for g in range(4):
            nc.sync.dma_start(
                out=scales[32 * g : 32 * g + 4, :].bitcast(I32),
                in_=cand_scales[0, 4 * g : 4 * g + 4, :].bitcast(I32),
            )
        with nc.allow_non_contiguous_dma(reason="one temperature a partition for each half"):
            nc.sync.dma_start(out=temps[:], in_=temp.rearrange("(h p) o -> p (h o)", h=HALVES))

        sought = [
            keep.tile([P, P, PACK], BF16, name="sought%d" % h, tag="sought%d" % h, align_bytes=64)
            for h in range(HALVES)
        ]

        def combine(h, t, picked_tag, diff_tag):
            cols = slice(h * LIST_COLS, (h + 1) * LIST_COLS)
            picked = keep.tile([P, P], F32, name="picked%d_%d" % (h, t), tag=picked_tag, align_bytes=64)
            diff = keep.tile([P, P], F32, name="diff%d_%d" % (h, t), tag=diff_tag, align_bytes=64)
            total = keep.tile([P, P], F32, name="total%d_%d" % (h, t))
            nc.vector.tensor_copy(picked[:], planes[t][:].indirect(second[:, cols]))
            nc.vector.tensor_tensor(diff[:], planes[t][:].indirect(third[:, cols]), picked[:], ALU.add)
            nc.vector.tensor_tensor(total[:], planes[t][:].indirect(first[:, cols]), diff[:], ALU.subtract)
            nc.scalar.activation(out=sought[h][:, :, t], in_=total[:], func=ACT.Copy, scale=feature_scale[:, t : t + 1])

        banks = {}

        def score(h, codes_tag):
            codes = keep.tile([P, P], U32, name="codes%d" % h, tag=codes_tag, align_bytes=64)
            code_scales = keep.tile([P, P], U8, name="code_scales%d" % h, align_bytes=64)
            nc.vector.quantize_mx(
                out=codes[:].bitcast(FP8X4),
                scales=code_scales[:],
                in_=sought[h][:].rearrange("p q t -> p (q t)"),
            )
            for c in range(CHUNKS):
                bank = psum.tile([P, BANK], F32, name="bank%d_%d" % (h, c))
                nc.tensor.matmul_mx(
                    out=bank[:],
                    lhsT=codes[:].bitcast(FP8X4),
                    lhsT_scale=code_scales[:],
                    rhs=words[:, 2 * BANK * c : 2 * BANK * (c + 1)].bitcast(FP4X4),
                    rhs_scale=scales[:, BANK * c : BANK * (c + 1)],
                    start=True,
                    stop=True,
                )
                banks[h, c] = bank

        for h, t in ((0, 0), (1, 0), (0, 1), (1, 1), (0, 3), (0, 2)):
            combine(h, t, "picked%d_%d" % (h, t), "diff%d_%d" % (h, t))

        inv_temp = keep.tile([P, HALVES], F32, name="inv_temp")
        nc.vector.reciprocal(inv_temp[:], temps[:])

        score(0, "codes0")
        combine(1, 3, "diff0_3", "diff1_3")
        combine(1, 2, "diff0_2", "sought0")

        pieces = [spans(widths) for widths in ((128, 384, 512, 512, 512), (512, 512, 512, 512))]
        neg_max = [keep.tile([P, len(pieces[h])], F32, name="neg_max%d" % h) for h in range(HALVES)]
        sums = [keep.tile([P, len(pieces[h])], F32, name="sums%d" % h) for h in range(HALVES)]
        factor = [keep.tile([P, len(pieces[h])], F32, name="factor%d" % h) for h in range(HALVES)]
        row_sum = [keep.tile([P, 1], F32, name="row_sum%d" % h) for h in range(HALVES)]
        norm = [keep.tile([P, 1], F32, name="norm%d" % h) for h in range(HALVES)]
        weights = {}

        def weigh(h, i):
            lo, hi = pieces[h][i]
            c = lo // BANK
            neg_s = keep.tile([P, hi - lo], F32, name="neg_s%d_%d" % (h, i), tag="neg_s%d_%d" % (h, i), align_bytes=64)
            weight = keep.tile([P, hi - lo], F32, name="weight%d_%d" % (h, i))
            nc.vector.tensor_scalar(
                neg_s[:], banks[h, c][:, lo - c * BANK : hi - c * BANK], inv_temp[:, h : h + 1], None,
                ALU.mult, ALU.min, accum_out=neg_max[h][:, i : i + 1],
            )
            if i == len(pieces[h]) - 1:
                row_neg_max = keep.tile([P, 1], F32, name="row_neg_max%d" % h)
                nc.vector.tensor_reduce(row_neg_max[:], neg_max[h][:], AX.X, ALU.min)
                nc.scalar.activation(
                    out=factor[h][:], in_=neg_max[h][:], func=ACT.Exp, bias=row_neg_max[:], scale=-1.0
                )
            nc.scalar.activation(
                out=weight[:], in_=neg_s[:], func=ACT.Exp, bias=neg_max[h][:, i : i + 1], scale=-1.0,
                accum_out=sums[h][:, i : i + 1],
            )
            weights[h, i] = weight

        def add_up(h):
            terms = keep.tile([P, len(pieces[h])], F32, name="terms%d" % h)
            nc.vector.scalar_tensor_tensor(
                terms[:], factor[h][:], 1.0 / OUT_SCALE, sums[h][:], ALU.mult, ALU.mult, accum_out=row_sum[h][:]
            )
            nc.vector.reciprocal(norm[h][:], row_sum[h][:])

        def finish(h, queue):
            for start, end in spans((512, 512, 1024)):
                result = keep.tile([P, end - start], F32, name="result%d_%d" % (h, start))
                for i, (lo, hi) in enumerate(pieces[h]):
                    if start <= lo < end:
                        nc.vector.tensor_scalar(
                            result[:, lo - start : hi - start], weights[h, i][:], factor[h][:, i : i + 1], norm[h][:],
                            ALU.mult, ALU.mult,
                        )
                queue.dma_start(out=out[h * P : (h + 1) * P, start:end], in_=result[:])

        weigh(0, 0)
        score(1, "neg_s0_0")
        for i in range(1, len(pieces[0])):
            weigh(0, i)
        add_up(0)
        for i in range(len(pieces[1])):
            weigh(1, i)
        add_up(1)
        finish(0, nc.sync)
        finish(1, nc.scalar)
